import numpy as np
import ml_dtypes

BF16 = ml_dtypes.bfloat16


def bf(x):
    return np.asarray(x, np.float32).astype(BF16)


def f32(x):
    return np.asarray(x, np.float32)


def f64(x):
    return np.asarray(x).astype(np.float64)


def striped(idx):
    return np.concatenate([l.reshape(-1, 16).T for l in idx])


def rows(idx, k):
    return np.tile(np.repeat(idx, 16, axis=0), (k // (16 * 8), 1))


def look(tab, idx):
    return np.take_along_axis(f64(tab), rows(idx, len(tab)), axis=1)


K, S, V, N, M = 512, 2048, 1024, 1024, 128


def setup_inputs():
    return {"tab": f32(np.random.standard_normal((2, K, S))), "w": bf(np.random.standard_normal((K, M)) / np.sqrt(K)), "b": f32(0.5 * np.random.standard_normal((M, 1))), "offs": striped(np.stack([np.random.permutation(S)[:N] for _ in range(8)]))}


def reference(tab, w, b, offs):
    idx = np.stack([g.T.reshape(-1) for g in np.split(offs, 8)])
    x = ((look(tab[0], idx) - 0.125) * 1.5) * (np.tanh(look(tab[1], idx)))
    return np.maximum(f64(w).T @ x + f64(b), 0.0)

@@ -1,0 +1,64 @@
+import concourse.mybir as mybir
+
+F32, BF16, U16 = mybir.dt.float32, mybir.dt.bfloat16, mybir.dt.uint16
+ALU = mybir.AluOpType
+ACT = mybir.ActivationFunctionType
+
+P = 128
+GROUP = 16
+PIECE = 512
+SHIFT, SCALE = 0.125, 1.5
+
+FLOPS = 2 * 512 * 128 * 1024
+
+
+def tile_lookup_vg_nrmtanh_relu_kernel(tc, tab, w, b, offs, out):
+    nc = tc.nc
+    rows, places = tab.shape[1:]
+    features, entries = out.shape
+    blocks, pieces = rows // P, entries // PIECE
+    offs_cols = PIECE // GROUP
+
+    with (
+        tc.tile_pool(name="held", bufs=1) as held,
+        tc.tile_pool(name="work", bufs=2 * pieces) as work,
+        tc.psum_pool(name="psum", bufs=1) as psum,
+    ):
+        offsets = held.tile([P, entries // GROUP], U16, name="offsets")
+        nc.sync.dma_start(offsets[:], offs)
+        weights = held.tile([P, blocks, features], BF16, name="weights")
+        nc.gpsimd.dma_start(weights[:], w.rearrange("(k p) m -> p k m", p=P))
+        bias = held.tile([features, 1], F32, name="bias")
+        nc.gpsimd.dma_start(bias[:], b)
+
+        value_windows, gate_windows = [], []
+        for k in range(blocks):
+            value_window = held.tile([P, places], F32, name=f"value_window{k}")
+            nc.sync.dma_start(value_window[:], tab[0, k * P : (k + 1) * P, :])
+            gate_window = held.tile([P, places], F32, name=f"gate_window{k}")
+            nc.sync.dma_start(gate_window[:], tab[1, k * P : (k + 1) * P, :])
+            value_windows.append(value_window)
+            gate_windows.append(gate_window)
+
+        sums = [psum.tile([features, PIECE], F32, name=f"sum{i}") for i in range(pieces)]
+        for k in range(blocks):
+            values, gates = [], []
+            for i in range(pieces):
+                piece = offsets[:, i * offs_cols : (i + 1) * offs_cols]
+                value = work.tile([P, PIECE], F32, name="value")
+                nc.vector.tensor_scalar(
+                    value[:], value_windows[k][:].indirect(piece), SHIFT, SCALE, ALU.subtract, ALU.mult
+                )
+                gate = work.tile([P, PIECE], F32, name="gate")
+                nc.scalar.activation(gate[:], gate_windows[k][:].indirect(piece), ACT.Tanh)
+                values.append(value)
+                gates.append(gate)
+            for i in range(pieces):
+                x = work.tile([P, PIECE], BF16, name="x")
+                nc.vector.tensor_tensor(x[:], values[i][:], gates[i][:], ALU.mult)
+                nc.tensor.matmul(sums[i][:], weights[:, k, :], x[:], start=(k == 0), stop=(k == blocks - 1))
+
+        for i in range(pieces):
+            result = work.tile([features, PIECE], F32, name="result")
+            nc.scalar.activation(result[:], sums[i][:], ACT.Relu, bias=bias[:])
+            nc.sync.dma_start(out[:, i * PIECE : (i + 1) * PIECE], result[:])

@@ -7,6 +7,7 @@ ACT = mybir.ActivationFunctionType
 P = 128
 GROUP = 16
 PIECE = 512
+CHUNK = 256
 SHIFT, SCALE = 0.125, 1.5
 
 FLOPS = 2 * 512 * 128 * 1024
@@ -16,20 +17,21 @@ def tile_lookup_vg_nrmtanh_relu_kernel(tc, tab, w, b, offs, out):
     nc = tc.nc
     rows, places = tab.shape[1:]
     features, entries = out.shape
-    blocks, pieces = rows // P, entries // PIECE
+    blocks, pieces, chunks = rows // P, entries // PIECE, entries // CHUNK
     offs_cols = PIECE // GROUP
 
     with (
         tc.tile_pool(name="held", bufs=1) as held,
         tc.tile_pool(name="work", bufs=2 * pieces) as work,
+        tc.tile_pool(name="narrow", bufs=blocks * chunks) as narrow,
         tc.psum_pool(name="psum", bufs=1) as psum,
     ):
         offsets = held.tile([P, entries // GROUP], U16, name="offsets")
         nc.sync.dma_start(offsets[:], offs)
         weights = held.tile([P, blocks, features], BF16, name="weights")
-        nc.gpsimd.dma_start(weights[:], w.rearrange("(k p) m -> p k m", p=P))
+        nc.scalar.dma_start(weights[:], w.rearrange("(k p) m -> p k m", p=P))
         bias = held.tile([features, 1], F32, name="bias")
-        nc.gpsimd.dma_start(bias[:], b)
+        nc.scalar.dma_start(bias[:], b)
 
         value_windows, gate_windows = [], []
         for k in range(blocks):
@@ -40,7 +42,7 @@ def tile_lookup_vg_nrmtanh_relu_kernel(tc, tab, w, b, offs, out):
             value_windows.append(value_window)
             gate_windows.append(gate_window)
 
-        sums = [psum.tile([features, PIECE], F32, name=f"sum{i}") for i in range(pieces)]
+        sums = [psum.tile([features, CHUNK], F32, name=f"sum{c}") for c in range(chunks)]
         for k in range(blocks):
             values, gates = [], []
             for i in range(pieces):
@@ -53,12 +55,14 @@ def tile_lookup_vg_nrmtanh_relu_kernel(tc, tab, w, b, offs, out):
                 nc.scalar.activation(gate[:], gate_windows[k][:].indirect(piece), ACT.Tanh)
                 values.append(value)
                 gates.append(gate)
-            for i in range(pieces):
-                x = work.tile([P, PIECE], BF16, name="x")
-                nc.vector.tensor_tensor(x[:], values[i][:], gates[i][:], ALU.mult)
-                nc.tensor.matmul(sums[i][:], weights[:, k, :], x[:], start=(k == 0), stop=(k == blocks - 1))
+            for c in range(chunks):
+                i, first = divmod(c * CHUNK, PIECE)
+                cols = slice(first, first + CHUNK)
+                x = narrow.tile([P, CHUNK], BF16, name="x")
+                nc.vector.tensor_tensor(x[:], values[i][:, cols], gates[i][:, cols], ALU.mult)
+                nc.tensor.matmul(sums[c][:], weights[:, k, :], x[:], start=(k == 0), stop=(k == blocks - 1))
 
-        for i in range(pieces):
-            result = work.tile([features, PIECE], F32, name="result")
-            nc.scalar.activation(result[:], sums[i][:], ACT.Relu, bias=bias[:])
-            nc.sync.dma_start(out[:, i * PIECE : (i + 1) * PIECE], result[:])
+        for c in range(chunks):
+            result = narrow.tile([features, CHUNK], F32, name="result")
+            nc.scalar.activation(result[:], sums[c][:], ACT.Relu, bias=bias[:])
+            nc.sync.dma_start(out[:, c * CHUNK : (c + 1) * CHUNK], result[:])

@@ -8,6 +8,7 @@ P = 128
 GROUP = 16
 PIECE = 512
 CHUNK = 256
+EARLY = 1
 SHIFT, SCALE = 0.125, 1.5
 
 FLOPS = 2 * 512 * 128 * 1024
@@ -26,21 +27,21 @@ def tile_lookup_vg_nrmtanh_relu_kernel(tc, tab, w, b, offs, out):
         tc.tile_pool(name="narrow", bufs=blocks * chunks) as narrow,
         tc.psum_pool(name="psum", bufs=1) as psum,
     ):
+        value_windows = [held.tile([P, places], F32, name=f"value_window{k}") for k in range(blocks)]
+        gate_windows = [held.tile([P, places], F32, name=f"gate_window{k}") for k in range(blocks)]
         offsets = held.tile([P, entries // GROUP], U16, name="offsets")
-        nc.sync.dma_start(offsets[:], offs)
         weights = held.tile([P, blocks, features], BF16, name="weights")
-        nc.scalar.dma_start(weights[:], w.rearrange("(k p) m -> p k m", p=P))
         bias = held.tile([features, 1], F32, name="bias")
-        nc.scalar.dma_start(bias[:], b)
+        w_blocks = w.rearrange("(k p) m -> p k m", p=P)
 
-        value_windows, gate_windows = [], []
+        nc.scalar.dma_start(weights[:, :EARLY, :], w_blocks[:, :EARLY, :])
         for k in range(blocks):
-            value_window = held.tile([P, places], F32, name=f"value_window{k}")
-            nc.sync.dma_start(value_window[:], tab[0, k * P : (k + 1) * P, :])
-            gate_window = held.tile([P, places], F32, name=f"gate_window{k}")
-            nc.sync.dma_start(gate_window[:], tab[1, k * P : (k + 1) * P, :])
-            value_windows.append(value_window)
-            gate_windows.append(gate_window)
+            nc.sync.dma_start(value_windows[k][:], tab[0, k * P : (k + 1) * P, :])
+            if k == 0:
+                nc.sync.dma_start(offsets[:], offs)
+            nc.sync.dma_start(gate_windows[k][:], tab[1, k * P : (k + 1) * P, :])
+        nc.sync.dma_start(weights[:, EARLY:, :], w_blocks[:, EARLY:, :])
+        nc.sync.dma_start(bias[:], b)
 
         sums = [psum.tile([features, CHUNK], F32, name=f"sum{c}") for c in range(chunks)]
         for k in range(blocks):

import concourse.mybir as mybir

F32, BF16, U16 = mybir.dt.float32, mybir.dt.bfloat16, mybir.dt.uint16
ALU = mybir.AluOpType
ACT = mybir.ActivationFunctionType

P = 128
GROUP = 16
PIECE = 512
CHUNK = 256
EARLY = 1
SHIFT, SCALE = 0.125, 1.5

FLOPS = 2 * 512 * 128 * 1024


def tile_lookup_vg_nrmtanh_relu_kernel(tc, tab, w, b, offs, out):
    nc = tc.nc
    rows, places = tab.shape[1:]
    features, entries = out.shape
    blocks, pieces, chunks = rows // P, entries // PIECE, entries // CHUNK
    offs_cols = PIECE // GROUP

    with (
        tc.tile_pool(name="held", bufs=1) as held,
        tc.tile_pool(name="work", bufs=2 * pieces) as work,
        tc.tile_pool(name="narrow", bufs=blocks * chunks) as narrow,
        tc.psum_pool(name="psum", bufs=1) as psum,
    ):
        value_windows = [held.tile([P, places], F32, name=f"value_window{k}") for k in range(blocks)]
        gate_windows = [held.tile([P, places], F32, name=f"gate_window{k}") for k in range(blocks)]
        offsets = held.tile([P, entries // GROUP], U16, name="offsets")
        weights = held.tile([P, blocks, features], BF16, name="weights")
        bias = held.tile([features, 1], F32, name="bias")
        w_blocks = w.rearrange("(k p) m -> p k m", p=P)

        nc.scalar.dma_start(weights[:, :EARLY, :], w_blocks[:, :EARLY, :])
        for k in range(blocks):
            nc.sync.dma_start(value_windows[k][:], tab[0, k * P : (k + 1) * P, :])
            if k == 0:
                nc.sync.dma_start(offsets[:], offs)
            nc.sync.dma_start(gate_windows[k][:], tab[1, k * P : (k + 1) * P, :])
        nc.sync.dma_start(weights[:, EARLY:, :], w_blocks[:, EARLY:, :])
        nc.sync.dma_start(bias[:], b)

        sums = [psum.tile([features, CHUNK], F32, name=f"sum{c}") for c in range(chunks)]
        for k in range(blocks):
            values, gates = [], []
            for i in range(pieces):
                piece = offsets[:, i * offs_cols : (i + 1) * offs_cols]
                value = work.tile([P, PIECE], F32, name="value")
                nc.vector.tensor_scalar(
                    value[:], value_windows[k][:].indirect(piece), SHIFT, SCALE, ALU.subtract, ALU.mult
                )
                gate = work.tile([P, PIECE], F32, name="gate")
                nc.scalar.activation(gate[:], gate_windows[k][:].indirect(piece), ACT.Tanh)
                values.append(value)
                gates.append(gate)
            for c in range(chunks):
                i, first = divmod(c * CHUNK, PIECE)
                cols = slice(first, first + CHUNK)
                x = narrow.tile([P, CHUNK], BF16, name="x")
                nc.vector.tensor_tensor(x[:], values[i][:, cols], gates[i][:, cols], ALU.mult)
                nc.tensor.matmul(sums[c][:], weights[:, k, :], x[:], start=(k == 0), stop=(k == blocks - 1))

        for c in range(chunks):
            result = narrow.tile([features, CHUNK], F32, name="result")
            nc.scalar.activation(result[:], sums[c][:], ACT.Relu, bias=bias[:])
            nc.sync.dma_start(out[:, c * CHUNK : (c + 1) * CHUNK], result[:])
